import numpy as np
import ml_dtypes


def mxq(x, axis, fmt="e4m3"):
    dtype, down = {"e4m3": (ml_dtypes.float8_e4m3fn, 7), "e5m2": (ml_dtypes.float8_e5m2, 14)}[fmt]
    v = np.moveaxis(np.asarray(x, np.float32).astype(ml_dtypes.bfloat16).astype(np.float64), axis, -1)
    blocks = v.reshape(v.shape[:-1] + (-1, 32))
    amax = np.abs(blocks).max(-1, keepdims=True)
    byte = np.maximum(np.where(amax > 0, np.frexp(amax)[1] - 1 + 127, 0) - down, 1)
    scale = np.exp2(byte - 127.0)
    codes = (blocks / scale).astype(np.float32).astype(dtype).astype(np.float64)
    return np.moveaxis((codes * scale).reshape(v.shape), -1, axis)


WIDE = False


def mx_kscale(k):
    if not WIDE:
        return np.ones(k)
    levels = np.array([10, -10, 5, -5, 0])
    if k % 512:
        return np.exp2(np.random.permutation(np.resize(levels, k // 32))).repeat(32)
    a = np.empty((k // 512, 16))
    for p in range(k // 512):
        a[p, :8] = np.random.permutation(np.resize(levels, 8))
        for g in range(8):
            far = levels[np.abs(levels - a[p, g]) >= 10]
            a[p, g + 8] = far[np.random.randint(len(far))]
    return np.exp2(a.ravel()).repeat(32)


def f64(x):
    return np.asarray(x).astype(np.float64)


def striped(idx):
    return np.tile(idx.reshape(-1, 16).T, (8, 1)).astype(np.uint16)


def unstriped(offs):
    return offs[:16].T.reshape(-1).astype(np.int64)


def pack_weight(w):
    k, n = w.shape
    w = f64(np.asarray(w, np.float32).astype(ml_dtypes.bfloat16)).reshape(k // 32, 32, n)
    amax = np.abs(w).max(1)
    byte = np.clip(np.where(amax > 0, np.frexp(amax)[1] - 1 + 127 - 7, 1), 1, 254)
    scaled = (w * np.exp2(127.0 - byte)[:, None, :]).reshape(k, n).astype(np.float32)
    words = np.ascontiguousarray(scaled.reshape(k // 512, 128, 4, n).transpose(0, 1, 3, 2)).astype(ml_dtypes.float8_e4m3fn).view(np.uint8)
    return words, np.ascontiguousarray(byte.astype(np.uint8).reshape(k // 512, 16, n))


def unpack_weight(words, scales):
    g, p, n, _ = words.shape
    vals = np.ascontiguousarray(words).view(ml_dtypes.float8_e4m3fn).astype(np.float64) * np.repeat(np.exp2(scales.astype(np.float64) - 127.0), 8, axis=1)[..., None]
    return vals.transpose(0, 1, 3, 2).reshape(g * 512, n)


def relu(v):
    return np.maximum(v, 0.0)


K, T, S, V, H, N = 1024, 1024, 512, 256, 512, 256


def setup_inputs():
    n = np.random.standard_normal
    s = mx_kscale(K)[:, None]
    u = mx_kscale(H)
    packed_w2 = pack_weight(n((H, N)) / np.sqrt(2 * H) / u[:, None])
    packed_w3 = pack_weight(n((H, N)) / np.sqrt(2 * H) / u[:, None])
    return {
        "xT": (n((K, T)) * s).astype(np.float32),
        "w1": (n((K, H)) / np.sqrt(K) / s * u).astype(np.float32),
        "w2_words": packed_w2[0],
        "w2_scales": packed_w2[1],
        "w3_words": packed_w3[0],
        "w3_scales": packed_w3[1],
        "offs": striped(np.random.permutation(T)[:S]),
        "cen": striped(np.random.permutation(S)[:V]),
        "pos1": striped(np.random.permutation(S)[:V]),
        "pos2": striped(np.random.permutation(S)[:V]),
    }


def reference(xT, w1, w2_words, w2_scales, w3_words, w3_scales, offs, cen, pos1, pos2):
    xq = mxq(f64(xT)[:, unstriped(offs)], 0, "e4m3")
    h = relu(mxq(f64(w1), 0, "e4m3").T @ xq)
    hc = h[:, unstriped(cen)]
    z = np.maximum(h[:, unstriped(pos1)], h[:, unstriped(pos2)])
    return relu(unpack_weight(w2_words, w2_scales).T @ mxq(hc, 0, "e4m3") + unpack_weight(w3_words, w3_scales).T @ mxq(z, 0, "e4m3"))

@@ -1,0 +1,182 @@
+from contextlib import ExitStack
+
+import concourse.mybir as mybir
+
+K, T, S, V, H, N = 1024, 1024, 512, 256, 512, 256
+FLOPS = 2 * K * H * S + 2 * 2 * H * N * V
+
+F32 = mybir.dt.float32
+BF16 = mybir.dt.bfloat16
+U32 = mybir.dt.uint32
+I32 = mybir.dt.int32
+U16 = mybir.dt.uint16
+U8 = mybir.dt.uint8
+FP8X4 = mybir.dt.float8_e4m3fn_x4
+RELU = mybir.ActivationFunctionType.Relu
+
+P = 128
+PACK = 4
+K_PASS = P * PACK
+PASSES = K // K_PASS
+X_VECTOR_NODES = (672, 672, 256, 384)
+W_VECTOR_COLUMNS = (16, 64)
+TILE_ORDER = (3, 2, 1, 0)
+
+
+def tile_picked_sagecat_maxrelu_e_kernel(
+    tc, xT, w1, w2_words, w2_scales, w3_words, w3_scales, offs, cen, pos1, pos2, out
+):
+    nc = tc.nc
+    with ExitStack() as ctx:
+        pool = ctx.enter_context(tc.tile_pool(name="sbuf", bufs=1))
+        psum = ctx.enter_context(tc.psum_pool(name="psum", bufs=1))
+
+        def sbuf(name, shape, dtype):
+            return pool.tile(shape, dtype, name=name, align_bytes=64)
+
+        offs_sb = sbuf("offs_sb", [P, S // 16], U16)
+        cen_sb = sbuf("cen_sb", [P, V // 16], U16)
+        pos1_sb = sbuf("pos1_sb", [P, V // 16], U16)
+        pos2_sb = sbuf("pos2_sb", [P, V // 16], U16)
+
+        w23_scales = sbuf("w23_scales", [P, 2 * N], U8)
+        nc.gpsimd.memset(w23_scales[:], 0)
+
+        def load_w1(g):
+            raw = sbuf(f"w1_raw{g}", [P, PACK, H], F32)
+            nc.sync.dma_start(out=raw[:], in_=w1[g * K_PASS : (g + 1) * K_PASS, :].rearrange("(p j) c -> p j c", j=PACK))
+            return raw
+
+        x_raw = {}
+        for g in range(PASSES):
+            rows = xT[g * K_PASS : (g + 1) * K_PASS, :].rearrange("(p j) t -> p j t", j=PACK)
+            for u in range(2):
+                x_raw[g, u] = sbuf(f"x_raw{g}{u}", [P, 2, T], F32)
+                nc.sync.dma_start(out=x_raw[g, u][:], in_=rows[:, 2 * u : 2 * u + 2, :])
+                if (g, u) == (0, 0):
+                    nc.sync.dma_start(offs_sb[:], offs)
+        w1_raw = [load_w1(g) for g in range(PASSES)]
+        nc.sync.dma_start(pos1_sb[:], pos1)
+        nc.sync.dma_start(pos2_sb[:], pos2)
+        nc.sync.dma_start(cen_sb[:], cen)
+        w2_codes = sbuf("w2_codes", [P, N], U32)
+        w3_codes = sbuf("w3_codes", [P, N], U32)
+        for codes, words in ((w3_codes, w3_words), (w2_codes, w2_words)):
+            nc.sync.dma_start(out=codes[:].bitcast(I32), in_=words[0].rearrange("p n r -> p (n r)").bitcast(I32))
+        for first, scales in ((N, w3_scales), (0, w2_scales)):
+            for q in range(4):
+                nc.sync.dma_start(
+                    out=w23_scales[32 * q : 32 * q + 4, first : first + N].bitcast(I32),
+                    in_=scales[0, 4 * q : 4 * q + 4, :].bitcast(I32),
+                )
+
+        x_grouped = [sbuf(f"x_grouped{g}", [P, PACK * S], BF16)[:] for g in range(PASSES)]
+        w1_grouped = [sbuf(f"w1_grouped{g}", [P, PACK * H], BF16)[:] for g in range(PASSES)]
+
+        def round_w1(g):
+            grouped_view = w1_grouped[g].rearrange("p (t m j) -> p m t j", t=PACK, j=PACK)
+            raw_view = w1_raw[g][:].rearrange("p j (m t) -> p m t j", t=PACK)
+            cut = W_VECTOR_COLUMNS[g]
+            nc.scalar.copy(out=grouped_view[:, cut:], in_=raw_view[:, cut:])
+            nc.vector.tensor_copy(out=grouped_view[:, :cut], in_=raw_view[:, :cut])
+
+
+        x_codes, x_scales = [], []
+        for g in range(PASSES):
+            picked = sbuf(f"picked{g}", [P, 2, S], U32)
+            for u in range(2):
+                cut = X_VECTOR_NODES[2 * g + u]
+                window = sbuf(f"pairs{g}{u}", [P, 2 * T], BF16)[:]
+                pairs_view = window.rearrange("p (t e) -> p t e", e=2)
+                raw_view = x_raw[g, u][:].rearrange("p e t -> p t e")
+                nc.scalar.copy(out=pairs_view[:, cut:, :], in_=raw_view[:, cut:, :])
+                nc.vector.tensor_copy(out=pairs_view[:, :cut, :], in_=raw_view[:, :cut, :])
+                nc.vector.tensor_copy(out=picked[:, u, :], in_=window.bitcast(U32).indirect(offs_sb[:]))
+            nc.vector.tensor_copy(
+                out=x_grouped[g].bitcast(F32).rearrange("p (s u) -> p s u", u=2),
+                in_=picked[:].bitcast(F32).rearrange("p u s -> p s u"),
+            )
+            x_codes.append(sbuf(f"x_codes{g}", [P, S], U32))
+            x_scales.append(sbuf(f"x_scales{g}", [P, S], U8))
+            nc.vector.quantize_mx(out=x_codes[g][:].bitcast(FP8X4), scales=x_scales[g][:], in_=x_grouped[g])
+
+        column_runs = {t: [(0, S)] for t in TILE_ORDER}
+        column_runs[TILE_ORDER[0]] = [(0, S // 2), (S // 2, S)]
+        acc = {}
+        for t in TILE_ORDER:
+            for a, b in column_runs[t]:
+                acc[t, a] = psum.tile([P, b - a], F32, name=f"acc{t}_{a}")
+        h = [sbuf(f"h{t}", [P, S], F32) for t in range(PACK)]
+
+        def multiply(t, g, codes, scales):
+            for a, b in column_runs[t]:
+                nc.tensor.matmul_mx(
+                    out=acc[t, a][:],
+                    lhsT=codes.bitcast(FP8X4),
+                    lhsT_scale=scales,
+                    rhs=x_codes[g][:, a:b].bitcast(FP8X4),
+                    rhs_scale=x_scales[g][:, a:b],
+                    start=(g == 0),
+                    stop=(g == PASSES - 1),
+                )
+
+        for t in TILE_ORDER:
+            for g in range(PASSES):
+                if t == TILE_ORDER[0]:
+                    round_w1(g)
+                w1_codes = sbuf(f"w1_codes{g}{t}", [P, P], U32)
+                w1_scales = sbuf(f"w1_scales{g}{t}", [P, P], U8)
+                nc.vector.quantize_mx(
+                    out=w1_codes[:].bitcast(FP8X4),
+                    scales=w1_scales[:],
+                    in_=w1_grouped[g][:, t * K_PASS : (t + 1) * K_PASS],
+                )
+                multiply(t, g, w1_codes[:], w1_scales[:])
+            for a, b in column_runs[t]:
+                if a > 0:
+                    nc.vector.tensor_scalar_max(out=h[t][:, a:b], in0=acc[t, a][:], scalar1=0.0)
+                else:
+                    nc.scalar.activation(out=h[t][:, a:b], in_=acc[t, a][:], func=RELU)
+
+        fetched = sbuf("fetched", [P, (PACK + 1) * V], BF16)
+        first = fetched[:, : PACK * V].rearrange("p (t v) -> p t v", t=PACK)
+        centre = fetched[:, V:].rearrange("p (t v) -> p t v", t=PACK)
+        second = sbuf("second", [P, PACK, V], BF16)
+        largest = sbuf("largest", [P, PACK, V], BF16)
+        for t in TILE_ORDER:
+            nc.vector.tensor_copy(out=first[:, t, :], in_=h[t][:].indirect(pos1_sb[:]))
+            nc.vector.tensor_copy(out=second[:, t, :], in_=h[t][:].indirect(pos2_sb[:]))
+        nc.vector.tensor_copy(out=centre[:, 3, :], in_=h[3][:].indirect(cen_sb[:]))
+        nc.vector.tensor_max(out=largest[:], in0=first, in1=second[:])
+        z_grouped = sbuf("z_grouped", [P, PACK * V], BF16)
+        nc.scalar.copy(out=z_grouped[:].rearrange("p (v t) -> p v t", t=PACK), in_=largest[:].rearrange("p t v -> p v t"))
+        for t in TILE_ORDER[1:]:
+            nc.vector.tensor_copy(out=centre[:, t, :], in_=h[t][:].indirect(cen_sb[:]))
+        c_grouped = sbuf("c_grouped", [P, PACK * V], BF16)
+        nc.vector.tensor_copy(out=c_grouped[:].rearrange("p (v t) -> p v t", t=PACK), in_=centre.rearrange("p t v -> p v t"))
+        z_codes = sbuf("z_codes", [P, V], U32)
+        z_scales = sbuf("z_scales", [P, V], U8)
+        nc.vector.quantize_mx(out=z_codes[:].bitcast(FP8X4), scales=z_scales[:], in_=z_grouped[:])
+        c_codes = sbuf("c_codes", [P, V], U32)
+        c_scales = sbuf("c_scales", [P, V], U8)
+        nc.vector.quantize_mx(out=c_codes[:].bitcast(FP8X4), scales=c_scales[:], in_=c_grouped[:])
+
+        sums = [psum.tile([P, V], F32, name=f"sums{b}") for b in range(N // P)]
+        operands = ((w3_codes, N, z_codes, z_scales), (w2_codes, 0, c_codes, c_scales))
+        for index, (w_codes, first_scale, codes, scales) in enumerate(operands):
+            for b in range(N // P):
+                nc.tensor.matmul_mx(
+                    out=sums[b][:],
+                    lhsT=w_codes[:, b * P : (b + 1) * P].bitcast(FP8X4),
+                    lhsT_scale=w23_scales[:, first_scale + b * P : first_scale + (b + 1) * P],
+                    rhs=codes[:].bitcast(FP8X4),
+                    rhs_scale=scales[:],
+                    start=(index == 0),
+                    stop=(index == 1),
+                )
+        result0 = sbuf("result0", [P, V], F32)
+        result1 = sbuf("result1", [P, V], F32)
+        nc.scalar.activation(out=result0[:], in_=sums[0][:], func=RELU)
+        nc.scalar.dma_start(out=out[0:P, :], in_=result0[:])
+        nc.vector.tensor_scalar_max(out=result1[:], in0=sums[1][:], scalar1=0.0)
+        nc.sync.dma_start(out=out[P : 2 * P, :], in_=result1[:])

@@ -18,8 +18,8 @@ P = 128
 PACK = 4
 K_PASS = P * PACK
 PASSES = K // K_PASS
-X_VECTOR_NODES = (672, 672, 256, 384)
-W_VECTOR_COLUMNS = (16, 64)
+X_VECTOR_NODES = (800, 576, 0, 384)
+W_VECTOR_COLUMNS = (32, 72)
 TILE_ORDER = (3, 2, 1, 0)
 
 
@@ -71,15 +71,9 @@ def tile_picked_sagecat_maxrelu_e_kernel(
                 )
 
         x_grouped = [sbuf(f"x_grouped{g}", [P, PACK * S], BF16)[:] for g in range(PASSES)]
-        w1_grouped = [sbuf(f"w1_grouped{g}", [P, PACK * H], BF16)[:] for g in range(PASSES)]
-
-        def round_w1(g):
-            grouped_view = w1_grouped[g].rearrange("p (t m j) -> p m t j", t=PACK, j=PACK)
-            raw_view = w1_raw[g][:].rearrange("p j (m t) -> p m t j", t=PACK)
-            cut = W_VECTOR_COLUMNS[g]
-            nc.scalar.copy(out=grouped_view[:, cut:], in_=raw_view[:, cut:])
-            nc.vector.tensor_copy(out=grouped_view[:, :cut], in_=raw_view[:, :cut])
-
+        w1_grouped = sbuf("w1_grouped", [P, PACK * PASSES * K_PASS], BF16)
+        grouped_view = w1_grouped[:].rearrange("p (t g m j) -> p g m t j", t=PACK, g=PASSES, j=PACK)
+        raw_views = [raw[:].rearrange("p j (m t) -> p m t j", t=PACK) for raw in w1_raw]
 
         x_codes, x_scales = [], []
         for g in range(PASSES):
@@ -90,7 +84,8 @@ def tile_picked_sagecat_maxrelu_e_kernel(
                 pairs_view = window.rearrange("p (t e) -> p t e", e=2)
                 raw_view = x_raw[g, u][:].rearrange("p e t -> p t e")
                 nc.scalar.copy(out=pairs_view[:, cut:, :], in_=raw_view[:, cut:, :])
-                nc.vector.tensor_copy(out=pairs_view[:, :cut, :], in_=raw_view[:, :cut, :])
+                if cut:
+                    nc.vector.tensor_copy(out=pairs_view[:, :cut, :], in_=raw_view[:, :cut, :])
                 nc.vector.tensor_copy(out=picked[:, u, :], in_=window.bitcast(U32).indirect(offs_sb[:]))
             nc.vector.tensor_copy(
                 out=x_grouped[g].bitcast(F32).rearrange("p (s u) -> p s u", u=2),
@@ -120,18 +115,27 @@ def tile_picked_sagecat_maxrelu_e_kernel(
                     stop=(g == PASSES - 1),
                 )
 
+        def quantise_and_multiply(t, passes):
+            width = len(passes) * P
+            start = (t * PASSES + passes[0]) * K_PASS
+            codes = sbuf(f"w1_codes{t}{passes[0]}", [P, width], U32)
+            scales = sbuf(f"w1_scales{t}{passes[0]}", [P, width], U8)
+            nc.vector.quantize_mx(
+                out=codes[:].bitcast(FP8X4), scales=scales[:], in_=w1_grouped[:, start : start + PACK * width]
+            )
+            for place, g in enumerate(passes):
+                multiply(t, g, codes[:, place * P : (place + 1) * P], scales[:, place * P : (place + 1) * P])
+
+        def round_w1(g):
+            cut = W_VECTOR_COLUMNS[g]
+            nc.scalar.copy(out=grouped_view[:, g, cut:], in_=raw_views[g][:, cut:])
+            nc.vector.tensor_copy(out=grouped_view[:, g, :cut], in_=raw_views[g][:, :cut])
+
+        round_w1(0)
+        quantise_and_multiply(TILE_ORDER[0], [0])
+        round_w1(1)
         for t in TILE_ORDER:
-            for g in range(PASSES):
-                if t == TILE_ORDER[0]:
-                    round_w1(g)
-                w1_codes = sbuf(f"w1_codes{g}{t}", [P, P], U32)
-                w1_scales = sbuf(f"w1_scales{g}{t}", [P, P], U8)
-                nc.vector.quantize_mx(
-                    out=w1_codes[:].bitcast(FP8X4),
-                    scales=w1_scales[:],
-                    in_=w1_grouped[g][:, t * K_PASS : (t + 1) * K_PASS],
-                )
-                multiply(t, g, w1_codes[:], w1_scales[:])
+            quantise_and_multiply(t, [1] if t == TILE_ORDER[0] else [0, 1])
             for a, b in column_runs[t]:
                 if a > 0:
                     nc.vector.tensor_scalar_max(out=h[t][:, a:b], in0=acc[t, a][:], scalar1=0.0)
@@ -139,18 +143,18 @@ def tile_picked_sagecat_maxrelu_e_kernel(
                     nc.scalar.activation(out=h[t][:, a:b], in_=acc[t, a][:], func=RELU)
 
         fetched = sbuf("fetched", [P, (PACK + 1) * V], BF16)
-        first = fetched[:, : PACK * V].rearrange("p (t v) -> p t v", t=PACK)
-        centre = fetched[:, V:].rearrange("p (t v) -> p t v", t=PACK)
+        first = fetched[:, V:].rearrange("p (t v) -> p t v", t=PACK)
+        centre = fetched[:, : PACK * V].rearrange("p (t v) -> p t v", t=PACK)
         second = sbuf("second", [P, PACK, V], BF16)
         largest = sbuf("largest", [P, PACK, V], BF16)
         for t in TILE_ORDER:
             nc.vector.tensor_copy(out=first[:, t, :], in_=h[t][:].indirect(pos1_sb[:]))
             nc.vector.tensor_copy(out=second[:, t, :], in_=h[t][:].indirect(pos2_sb[:]))
-        nc.vector.tensor_copy(out=centre[:, 3, :], in_=h[3][:].indirect(cen_sb[:]))
+        nc.vector.tensor_copy(out=centre[:, 0, :], in_=h[0][:].indirect(cen_sb[:]))
         nc.vector.tensor_max(out=largest[:], in0=first, in1=second[:])
         z_grouped = sbuf("z_grouped", [P, PACK * V], BF16)
         nc.scalar.copy(out=z_grouped[:].rearrange("p (v t) -> p v t", t=PACK), in_=largest[:].rearrange("p t v -> p v t"))
-        for t in TILE_ORDER[1:]:
+        for t in TILE_ORDER[:-1]:
             nc.vector.tensor_copy(out=centre[:, t, :], in_=h[t][:].indirect(cen_sb[:]))
         c_grouped = sbuf("c_grouped", [P, PACK * V], BF16)
         nc.vector.tensor_copy(out=c_grouped[:].rearrange("p (v t) -> p v t", t=PACK), in_=centre.rearrange("p t v -> p v t"))

@@ -18,9 +18,12 @@ P = 128
 PACK = 4
 K_PASS = P * PACK
 PASSES = K // K_PASS
-X_VECTOR_NODES = (800, 576, 0, 384)
-W_VECTOR_COLUMNS = (32, 72)
-TILE_ORDER = (3, 2, 1, 0)
+LIST_ROWS = 16
+QUADRANT = 32
+
+X_VECTOR_NODES = (576, 512, 128, 384)
+W_VECTOR_COLUMNS = (40, 72)
+C_VECTOR_TARGETS = 160
 
 
 def tile_picked_sagecat_maxrelu_e_kernel(
@@ -34,27 +37,47 @@ def tile_picked_sagecat_maxrelu_e_kernel(
         def sbuf(name, shape, dtype):
             return pool.tile(shape, dtype, name=name, align_bytes=64)
 
-        offs_sb = sbuf("offs_sb", [P, S // 16], U16)
-        cen_sb = sbuf("cen_sb", [P, V // 16], U16)
-        pos1_sb = sbuf("pos1_sb", [P, V // 16], U16)
-        pos2_sb = sbuf("pos2_sb", [P, V // 16], U16)
+        def quantise(name, values):
+            words = values.shape[1] // PACK
+            codes = sbuf(name + "_codes", [P, words], U32)
+            scales = sbuf(name + "_scales", [P, words], U8)
+            nc.vector.quantize_mx(out=codes[:].bitcast(FP8X4), scales=scales[:], in_=values)
+            return codes, scales
+
+        def multiply(sums, stationary, moving, start, stop):
+            nc.tensor.matmul_mx(
+                out=sums,
+                lhsT=stationary[0].bitcast(FP8X4),
+                lhsT_scale=stationary[1],
+                rhs=moving[0].bitcast(FP8X4),
+                rhs_scale=moving[1],
+                start=start,
+                stop=stop,
+            )
+
+        offs_sb = sbuf("offs_sb", [P, S // LIST_ROWS], U16)
+        cen_sb = sbuf("cen_sb", [P, V // LIST_ROWS], U16)
+        pos1_sb = sbuf("pos1_sb", [P, V // LIST_ROWS], U16)
+        pos2_sb = sbuf("pos2_sb", [P, V // LIST_ROWS], U16)
 
         w23_scales = sbuf("w23_scales", [P, 2 * N], U8)
         nc.gpsimd.memset(w23_scales[:], 0)
+
+        def load_x(g, u):
+            raw = sbuf(f"x_raw{g}{u}", [P, 2, T], F32)
+            rows = xT[g * K_PASS : (g + 1) * K_PASS, :].rearrange("(p j) t -> p j t", j=PACK)
+            nc.sync.dma_start(out=raw[:], in_=rows[:, 2 * u : 2 * u + 2, :])
+            return raw
 
         def load_w1(g):
             raw = sbuf(f"w1_raw{g}", [P, PACK, H], F32)
             nc.sync.dma_start(out=raw[:], in_=w1[g * K_PASS : (g + 1) * K_PASS, :].rearrange("(p j) c -> p j c", j=PACK))
             return raw
 
-        x_raw = {}
-        for g in range(PASSES):
-            rows = xT[g * K_PASS : (g + 1) * K_PASS, :].rearrange("(p j) t -> p j t", j=PACK)
-            for u in range(2):
-                x_raw[g, u] = sbuf(f"x_raw{g}{u}", [P, 2, T], F32)
-                nc.sync.dma_start(out=x_raw[g, u][:], in_=rows[:, 2 * u : 2 * u + 2, :])
-                if (g, u) == (0, 0):
-                    nc.sync.dma_start(offs_sb[:], offs)
+        x_raw = {(0, 0): load_x(0, 0)}
+        nc.sync.dma_start(offs_sb[:], offs)
+        for g, u in ((0, 1), (1, 0), (1, 1)):
+            x_raw[g, u] = load_x(g, u)
         w1_raw = [load_w1(g) for g in range(PASSES)]
         nc.sync.dma_start(pos1_sb[:], pos1)
         nc.sync.dma_start(pos2_sb[:], pos2)
@@ -63,124 +86,100 @@ def tile_picked_sagecat_maxrelu_e_kernel(
         w3_codes = sbuf("w3_codes", [P, N], U32)
         for codes, words in ((w3_codes, w3_words), (w2_codes, w2_words)):
             nc.sync.dma_start(out=codes[:].bitcast(I32), in_=words[0].rearrange("p n r -> p (n r)").bitcast(I32))
-        for first, scales in ((N, w3_scales), (0, w2_scales)):
-            for q in range(4):
+        for first_column, scale_rows in ((N, w3_scales), (0, w2_scales)):
+            for q in range(P // QUADRANT):
                 nc.sync.dma_start(
-                    out=w23_scales[32 * q : 32 * q + 4, first : first + N].bitcast(I32),
-                    in_=scales[0, 4 * q : 4 * q + 4, :].bitcast(I32),
+                    out=w23_scales[QUADRANT * q : QUADRANT * q + 4, first_column : first_column + N].bitcast(I32),
+                    in_=scale_rows[0, 4 * q : 4 * q + 4, :].bitcast(I32),
                 )
 
-        x_grouped = [sbuf(f"x_grouped{g}", [P, PACK * S], BF16)[:] for g in range(PASSES)]
-        w1_grouped = sbuf("w1_grouped", [P, PACK * PASSES * K_PASS], BF16)
-        grouped_view = w1_grouped[:].rearrange("p (t g m j) -> p g m t j", t=PACK, g=PASSES, j=PACK)
-        raw_views = [raw[:].rearrange("p j (m t) -> p m t j", t=PACK) for raw in w1_raw]
-
-        x_codes, x_scales = [], []
-        for g in range(PASSES):
+        def picked_nodes(g):
             picked = sbuf(f"picked{g}", [P, 2, S], U32)
             for u in range(2):
+                pairs = sbuf(f"pairs{g}{u}", [P, 2 * T], BF16)
+                by_node = pairs[:].rearrange("p (t e) -> p t e", e=2)
+                raw_by_node = x_raw[g, u][:].rearrange("p e t -> p t e")
                 cut = X_VECTOR_NODES[2 * g + u]
-                window = sbuf(f"pairs{g}{u}", [P, 2 * T], BF16)[:]
-                pairs_view = window.rearrange("p (t e) -> p t e", e=2)
-                raw_view = x_raw[g, u][:].rearrange("p e t -> p t e")
-                nc.scalar.copy(out=pairs_view[:, cut:, :], in_=raw_view[:, cut:, :])
-                if cut:
-                    nc.vector.tensor_copy(out=pairs_view[:, :cut, :], in_=raw_view[:, :cut, :])
-                nc.vector.tensor_copy(out=picked[:, u, :], in_=window.bitcast(U32).indirect(offs_sb[:]))
+                nc.scalar.copy(out=by_node[:, cut:, :], in_=raw_by_node[:, cut:, :])
+                nc.vector.tensor_copy(out=by_node[:, :cut, :], in_=raw_by_node[:, :cut, :])
+                nc.vector.tensor_copy(out=picked[:, u, :], in_=pairs[:].bitcast(U32).indirect(offs_sb[:]))
+            woven = sbuf(f"x_woven{g}", [P, PACK * S], BF16)
             nc.vector.tensor_copy(
-                out=x_grouped[g].bitcast(F32).rearrange("p (s u) -> p s u", u=2),
+                out=woven[:].bitcast(F32).rearrange("p (s u) -> p s u", u=2),
                 in_=picked[:].bitcast(F32).rearrange("p u s -> p s u"),
             )
-            x_codes.append(sbuf(f"x_codes{g}", [P, S], U32))
-            x_scales.append(sbuf(f"x_scales{g}", [P, S], U8))
-            nc.vector.quantize_mx(out=x_codes[g][:].bitcast(FP8X4), scales=x_scales[g][:], in_=x_grouped[g])
+            return quantise(f"x{g}", woven[:])
 
-        column_runs = {t: [(0, S)] for t in TILE_ORDER}
-        column_runs[TILE_ORDER[0]] = [(0, S // 2), (S // 2, S)]
-        acc = {}
-        for t in TILE_ORDER:
-            for a, b in column_runs[t]:
-                acc[t, a] = psum.tile([P, b - a], F32, name=f"acc{t}_{a}")
-        h = [sbuf(f"h{t}", [P, S], F32) for t in range(PACK)]
-
-        def multiply(t, g, codes, scales):
-            for a, b in column_runs[t]:
-                nc.tensor.matmul_mx(
-                    out=acc[t, a][:],
-                    lhsT=codes.bitcast(FP8X4),
-                    lhsT_scale=scales,
-                    rhs=x_codes[g][:, a:b].bitcast(FP8X4),
-                    rhs_scale=x_scales[g][:, a:b],
-                    start=(g == 0),
-                    stop=(g == PASSES - 1),
-                )
-
-        def quantise_and_multiply(t, passes):
-            width = len(passes) * P
-            start = (t * PASSES + passes[0]) * K_PASS
-            codes = sbuf(f"w1_codes{t}{passes[0]}", [P, width], U32)
-            scales = sbuf(f"w1_scales{t}{passes[0]}", [P, width], U8)
-            nc.vector.quantize_mx(
-                out=codes[:].bitcast(FP8X4), scales=scales[:], in_=w1_grouped[:, start : start + PACK * width]
-            )
-            for place, g in enumerate(passes):
-                multiply(t, g, codes[:, place * P : (place + 1) * P], scales[:, place * P : (place + 1) * P])
-
-        def round_w1(g):
+        def rounded_w1(g):
+            rounded = sbuf(f"w1_rounded{g}", [P, PACK * H], BF16)
+            dealt = rounded[:].rearrange("p (t m j) -> p m t j", t=PACK, j=PACK)
+            raw = w1_raw[g][:].rearrange("p j (m t) -> p m t j", t=PACK)
             cut = W_VECTOR_COLUMNS[g]
-            nc.scalar.copy(out=grouped_view[:, g, cut:], in_=raw_views[g][:, cut:])
-            nc.vector.tensor_copy(out=grouped_view[:, g, :cut], in_=raw_views[g][:, :cut])
+            nc.scalar.copy(out=dealt[:, cut:], in_=raw[:, cut:])
+            nc.vector.tensor_copy(out=dealt[:, :cut], in_=raw[:, :cut])
+            return rounded
 
-        round_w1(0)
-        quantise_and_multiply(TILE_ORDER[0], [0])
-        round_w1(1)
-        for t in TILE_ORDER:
-            quantise_and_multiply(t, [1] if t == TILE_ORDER[0] else [0, 1])
-            for a, b in column_runs[t]:
-                if a > 0:
-                    nc.vector.tensor_scalar_max(out=h[t][:, a:b], in0=acc[t, a][:], scalar1=0.0)
+        nodes = [picked_nodes(g) for g in range(PASSES)]
+
+        entry_runs = [[slice(0, S // 2), slice(S // 2, S)]] + [[slice(0, S)]] * (PACK - 1)
+        banks = [[0, 1], [2], [0], [1]]
+        h = [sbuf(f"h{t}", [P, S], F32) for t in range(PACK)]
+        w1_rounded = []
+        for t in range(PACK):
+            h_sums = [
+                psum.tile([P, run.stop - run.start], F32, name=f"h_sums{t}_{bank}", tag=f"h_bank{bank}")
+                for run, bank in zip(entry_runs[t], banks[t])
+            ]
+            for g in range(PASSES):
+                if t == 0:
+                    w1_rounded.append(rounded_w1(g))
+                codes, scales = quantise(f"w1_{g}{t}", w1_rounded[g][:, t * K_PASS : (t + 1) * K_PASS])
+                for sums, run in zip(h_sums, entry_runs[t]):
+                    moving = (nodes[g][0][:, run], nodes[g][1][:, run])
+                    multiply(sums[:], (codes[:], scales[:]), moving, g == 0, g == PASSES - 1)
+            for sums, run in zip(h_sums, entry_runs[t]):
+                if t == 0:
+                    nc.vector.tensor_scalar_max(out=h[t][:, run], in0=sums[:], scalar1=0.0)
                 else:
-                    nc.scalar.activation(out=h[t][:, a:b], in_=acc[t, a][:], func=RELU)
+                    nc.scalar.activation(out=h[t][:, run], in_=sums[:], func=RELU)
 
         fetched = sbuf("fetched", [P, (PACK + 1) * V], BF16)
         first = fetched[:, V:].rearrange("p (t v) -> p t v", t=PACK)
-        centre = fetched[:, : PACK * V].rearrange("p (t v) -> p t v", t=PACK)
+        centres = fetched[:, : PACK * V].rearrange("p (t v) -> p t v", t=PACK)
         second = sbuf("second", [P, PACK, V], BF16)
         largest = sbuf("largest", [P, PACK, V], BF16)
-        for t in TILE_ORDER:
+        for t in range(PACK):
             nc.vector.tensor_copy(out=first[:, t, :], in_=h[t][:].indirect(pos1_sb[:]))
             nc.vector.tensor_copy(out=second[:, t, :], in_=h[t][:].indirect(pos2_sb[:]))
-        nc.vector.tensor_copy(out=centre[:, 0, :], in_=h[0][:].indirect(cen_sb[:]))
+            if t == 0:
+                nc.vector.tensor_copy(out=centres[:, t, :], in_=h[t][:].indirect(cen_sb[:]))
         nc.vector.tensor_max(out=largest[:], in0=first, in1=second[:])
-        z_grouped = sbuf("z_grouped", [P, PACK * V], BF16)
-        nc.scalar.copy(out=z_grouped[:].rearrange("p (v t) -> p v t", t=PACK), in_=largest[:].rearrange("p t v -> p v t"))
-        for t in TILE_ORDER[:-1]:
-            nc.vector.tensor_copy(out=centre[:, t, :], in_=h[t][:].indirect(cen_sb[:]))
-        c_grouped = sbuf("c_grouped", [P, PACK * V], BF16)
-        nc.vector.tensor_copy(out=c_grouped[:].rearrange("p (v t) -> p v t", t=PACK), in_=centre.rearrange("p t v -> p v t"))
-        z_codes = sbuf("z_codes", [P, V], U32)
-        z_scales = sbuf("z_scales", [P, V], U8)
-        nc.vector.quantize_mx(out=z_codes[:].bitcast(FP8X4), scales=z_scales[:], in_=z_grouped[:])
-        c_codes = sbuf("c_codes", [P, V], U32)
-        c_scales = sbuf("c_scales", [P, V], U8)
-        nc.vector.quantize_mx(out=c_codes[:].bitcast(FP8X4), scales=c_scales[:], in_=c_grouped[:])
 
-        sums = [psum.tile([P, V], F32, name=f"sums{b}") for b in range(N // P)]
-        operands = ((w3_codes, N, z_codes, z_scales), (w2_codes, 0, c_codes, c_scales))
-        for index, (w_codes, first_scale, codes, scales) in enumerate(operands):
-            for b in range(N // P):
-                nc.tensor.matmul_mx(
-                    out=sums[b][:],
-                    lhsT=w_codes[:, b * P : (b + 1) * P].bitcast(FP8X4),
-                    lhsT_scale=w23_scales[:, first_scale + b * P : first_scale + (b + 1) * P],
-                    rhs=codes[:].bitcast(FP8X4),
-                    rhs_scale=scales[:],
-                    start=(index == 0),
-                    stop=(index == 1),
-                )
-        result0 = sbuf("result0", [P, V], F32)
-        result1 = sbuf("result1", [P, V], F32)
-        nc.scalar.activation(out=result0[:], in_=sums[0][:], func=RELU)
-        nc.scalar.dma_start(out=out[0:P, :], in_=result0[:])
-        nc.vector.tensor_scalar_max(out=result1[:], in0=sums[1][:], scalar1=0.0)
-        nc.sync.dma_start(out=out[P : 2 * P, :], in_=result1[:])
+        centre_start = PACK * (V - C_VECTOR_TARGETS)
+        by_target = sbuf("by_target", [P, centre_start + PACK * V], BF16)
+        z_values = by_target[:, : PACK * V]
+        centre_values = by_target[:, centre_start:]
+        nc.scalar.copy(out=z_values.rearrange("p (v t) -> p v t", t=PACK), in_=largest[:].rearrange("p t v -> p v t"))
+        for t in range(1, PACK):
+            nc.vector.tensor_copy(out=centres[:, t, :], in_=h[t][:].indirect(cen_sb[:]))
+        z_codes, z_scales = quantise("z", z_values)
+        dealt_centres = centre_values.rearrange("p (v t) -> p v t", t=PACK)
+        centres_by_target = centres.rearrange("p t v -> p v t")
+        nc.scalar.copy(out=dealt_centres[:, C_VECTOR_TARGETS:], in_=centres_by_target[:, C_VECTOR_TARGETS:])
+        nc.vector.tensor_copy(out=dealt_centres[:, :C_VECTOR_TARGETS], in_=centres_by_target[:, :C_VECTOR_TARGETS])
+        centre_codes, centre_scales = quantise("centre", centre_values)
+
+        out_sums = [psum.tile([P, V], F32, name=f"out_sums{b}") for b in range(N // P)]
+        for b in range(N // P):
+            stationary = (w3_codes[:, b * P : (b + 1) * P], w23_scales[:, N + b * P : N + (b + 1) * P])
+            multiply(out_sums[b][:], stationary, (z_codes[:], z_scales[:]), True, False)
+        for b in range(N // P):
+            stationary = (w2_codes[:, b * P : (b + 1) * P], w23_scales[:, b * P : (b + 1) * P])
+            multiply(out_sums[b][:], stationary, (centre_codes[:], centre_scales[:]), False, True)
+
+        upper = sbuf("upper", [P, V], F32)
+        lower = sbuf("lower", [P, V], F32)
+        nc.scalar.activation(out=upper[:], in_=out_sums[0][:], func=RELU)
+        nc.scalar.dma_start(out=out[0:P, :], in_=upper[:])
+        nc.vector.tensor_scalar_max(out=lower[:], in0=out_sums[1][:], scalar1=0.0)
+        nc.sync.dma_start(out=out[P : 2 * P, :], in_=lower[:])

from contextlib import ExitStack

import concourse.mybir as mybir

K, T, S, V, H, N = 1024, 1024, 512, 256, 512, 256
FLOPS = 2 * K * H * S + 2 * 2 * H * N * V

F32 = mybir.dt.float32
BF16 = mybir.dt.bfloat16
U32 = mybir.dt.uint32
I32 = mybir.dt.int32
U16 = mybir.dt.uint16
U8 = mybir.dt.uint8
FP8X4 = mybir.dt.float8_e4m3fn_x4
RELU = mybir.ActivationFunctionType.Relu

P = 128
PACK = 4
K_PASS = P * PACK
PASSES = K // K_PASS
LIST_ROWS = 16
QUADRANT = 32

X_VECTOR_NODES = (576, 512, 128, 384)
W_VECTOR_COLUMNS = (40, 72)
C_VECTOR_TARGETS = 160


def tile_picked_sagecat_maxrelu_e_kernel(
    tc, xT, w1, w2_words, w2_scales, w3_words, w3_scales, offs, cen, pos1, pos2, out
):
    nc = tc.nc
    with ExitStack() as ctx:
        pool = ctx.enter_context(tc.tile_pool(name="sbuf", bufs=1))
        psum = ctx.enter_context(tc.psum_pool(name="psum", bufs=1))

        def sbuf(name, shape, dtype):
            return pool.tile(shape, dtype, name=name, align_bytes=64)

        def quantise(name, values):
            words = values.shape[1] // PACK
            codes = sbuf(name + "_codes", [P, words], U32)
            scales = sbuf(name + "_scales", [P, words], U8)
            nc.vector.quantize_mx(out=codes[:].bitcast(FP8X4), scales=scales[:], in_=values)
            return codes, scales

        def multiply(sums, stationary, moving, start, stop):
            nc.tensor.matmul_mx(
                out=sums,
                lhsT=stationary[0].bitcast(FP8X4),
                lhsT_scale=stationary[1],
                rhs=moving[0].bitcast(FP8X4),
                rhs_scale=moving[1],
                start=start,
                stop=stop,
            )

        offs_sb = sbuf("offs_sb", [P, S // LIST_ROWS], U16)
        cen_sb = sbuf("cen_sb", [P, V // LIST_ROWS], U16)
        pos1_sb = sbuf("pos1_sb", [P, V // LIST_ROWS], U16)
        pos2_sb = sbuf("pos2_sb", [P, V // LIST_ROWS], U16)

        w23_scales = sbuf("w23_scales", [P, 2 * N], U8)
        nc.gpsimd.memset(w23_scales[:], 0)

        def load_x(g, u):
            raw = sbuf(f"x_raw{g}{u}", [P, 2, T], F32)
            rows = xT[g * K_PASS : (g + 1) * K_PASS, :].rearrange("(p j) t -> p j t", j=PACK)
            nc.sync.dma_start(out=raw[:], in_=rows[:, 2 * u : 2 * u + 2, :])
            return raw

        def load_w1(g):
            raw = sbuf(f"w1_raw{g}", [P, PACK, H], F32)
            nc.sync.dma_start(out=raw[:], in_=w1[g * K_PASS : (g + 1) * K_PASS, :].rearrange("(p j) c -> p j c", j=PACK))
            return raw

        x_raw = {(0, 0): load_x(0, 0)}
        nc.sync.dma_start(offs_sb[:], offs)
        for g, u in ((0, 1), (1, 0), (1, 1)):
            x_raw[g, u] = load_x(g, u)
        w1_raw = [load_w1(g) for g in range(PASSES)]
        nc.sync.dma_start(pos1_sb[:], pos1)
        nc.sync.dma_start(pos2_sb[:], pos2)
        nc.sync.dma_start(cen_sb[:], cen)
        w2_codes = sbuf("w2_codes", [P, N], U32)
        w3_codes = sbuf("w3_codes", [P, N], U32)
        for codes, words in ((w3_codes, w3_words), (w2_codes, w2_words)):
            nc.sync.dma_start(out=codes[:].bitcast(I32), in_=words[0].rearrange("p n r -> p (n r)").bitcast(I32))
        for first_column, scale_rows in ((N, w3_scales), (0, w2_scales)):
            for q in range(P // QUADRANT):
                nc.sync.dma_start(
                    out=w23_scales[QUADRANT * q : QUADRANT * q + 4, first_column : first_column + N].bitcast(I32),
                    in_=scale_rows[0, 4 * q : 4 * q + 4, :].bitcast(I32),
                )

        def picked_nodes(g):
            picked = sbuf(f"picked{g}", [P, 2, S], U32)
            for u in range(2):
                pairs = sbuf(f"pairs{g}{u}", [P, 2 * T], BF16)
                by_node = pairs[:].rearrange("p (t e) -> p t e", e=2)
                raw_by_node = x_raw[g, u][:].rearrange("p e t -> p t e")
                cut = X_VECTOR_NODES[2 * g + u]
                nc.scalar.copy(out=by_node[:, cut:, :], in_=raw_by_node[:, cut:, :])
                nc.vector.tensor_copy(out=by_node[:, :cut, :], in_=raw_by_node[:, :cut, :])
                nc.vector.tensor_copy(out=picked[:, u, :], in_=pairs[:].bitcast(U32).indirect(offs_sb[:]))
            woven = sbuf(f"x_woven{g}", [P, PACK * S], BF16)
            nc.vector.tensor_copy(
                out=woven[:].bitcast(F32).rearrange("p (s u) -> p s u", u=2),
                in_=picked[:].bitcast(F32).rearrange("p u s -> p s u"),
            )
            return quantise(f"x{g}", woven[:])

        def rounded_w1(g):
            rounded = sbuf(f"w1_rounded{g}", [P, PACK * H], BF16)
            dealt = rounded[:].rearrange("p (t m j) -> p m t j", t=PACK, j=PACK)
            raw = w1_raw[g][:].rearrange("p j (m t) -> p m t j", t=PACK)
            cut = W_VECTOR_COLUMNS[g]
            nc.scalar.copy(out=dealt[:, cut:], in_=raw[:, cut:])
            nc.vector.tensor_copy(out=dealt[:, :cut], in_=raw[:, :cut])
            return rounded

        nodes = [picked_nodes(g) for g in range(PASSES)]

        entry_runs = [[slice(0, S // 2), slice(S // 2, S)]] + [[slice(0, S)]] * (PACK - 1)
        banks = [[0, 1], [2], [0], [1]]
        h = [sbuf(f"h{t}", [P, S], F32) for t in range(PACK)]
        w1_rounded = []
        for t in range(PACK):
            h_sums = [
                psum.tile([P, run.stop - run.start], F32, name=f"h_sums{t}_{bank}", tag=f"h_bank{bank}")
                for run, bank in zip(entry_runs[t], banks[t])
            ]
            for g in range(PASSES):
                if t == 0:
                    w1_rounded.append(rounded_w1(g))
                codes, scales = quantise(f"w1_{g}{t}", w1_rounded[g][:, t * K_PASS : (t + 1) * K_PASS])
                for sums, run in zip(h_sums, entry_runs[t]):
                    moving = (nodes[g][0][:, run], nodes[g][1][:, run])
                    multiply(sums[:], (codes[:], scales[:]), moving, g == 0, g == PASSES - 1)
            for sums, run in zip(h_sums, entry_runs[t]):
                if t == 0:
                    nc.vector.tensor_scalar_max(out=h[t][:, run], in0=sums[:], scalar1=0.0)
                else:
                    nc.scalar.activation(out=h[t][:, run], in_=sums[:], func=RELU)

        fetched = sbuf("fetched", [P, (PACK + 1) * V], BF16)
        first = fetched[:, V:].rearrange("p (t v) -> p t v", t=PACK)
        centres = fetched[:, : PACK * V].rearrange("p (t v) -> p t v", t=PACK)
        second = sbuf("second", [P, PACK, V], BF16)
        largest = sbuf("largest", [P, PACK, V], BF16)
        for t in range(PACK):
            nc.vector.tensor_copy(out=first[:, t, :], in_=h[t][:].indirect(pos1_sb[:]))
            nc.vector.tensor_copy(out=second[:, t, :], in_=h[t][:].indirect(pos2_sb[:]))
            if t == 0:
                nc.vector.tensor_copy(out=centres[:, t, :], in_=h[t][:].indirect(cen_sb[:]))
        nc.vector.tensor_max(out=largest[:], in0=first, in1=second[:])

        centre_start = PACK * (V - C_VECTOR_TARGETS)
        by_target = sbuf("by_target", [P, centre_start + PACK * V], BF16)
        z_values = by_target[:, : PACK * V]
        centre_values = by_target[:, centre_start:]
        nc.scalar.copy(out=z_values.rearrange("p (v t) -> p v t", t=PACK), in_=largest[:].rearrange("p t v -> p v t"))
        for t in range(1, PACK):
            nc.vector.tensor_copy(out=centres[:, t, :], in_=h[t][:].indirect(cen_sb[:]))
        z_codes, z_scales = quantise("z", z_values)
        dealt_centres = centre_values.rearrange("p (v t) -> p v t", t=PACK)
        centres_by_target = centres.rearrange("p t v -> p v t")
        nc.scalar.copy(out=dealt_centres[:, C_VECTOR_TARGETS:], in_=centres_by_target[:, C_VECTOR_TARGETS:])
        nc.vector.tensor_copy(out=dealt_centres[:, :C_VECTOR_TARGETS], in_=centres_by_target[:, :C_VECTOR_TARGETS])
        centre_codes, centre_scales = quantise("centre", centre_values)

        out_sums = [psum.tile([P, V], F32, name=f"out_sums{b}") for b in range(N // P)]
        for b in range(N // P):
            stationary = (w3_codes[:, b * P : (b + 1) * P], w23_scales[:, N + b * P : N + (b + 1) * P])
            multiply(out_sums[b][:], stationary, (z_codes[:], z_scales[:]), True, False)
        for b in range(N // P):
            stationary = (w2_codes[:, b * P : (b + 1) * P], w23_scales[:, b * P : (b + 1) * P])
            multiply(out_sums[b][:], stationary, (centre_codes[:], centre_scales[:]), False, True)

        upper = sbuf("upper", [P, V], F32)
        lower = sbuf("lower", [P, V], F32)
        nc.scalar.activation(out=upper[:], in_=out_sums[0][:], func=RELU)
        nc.scalar.dma_start(out=out[0:P, :], in_=upper[:])
        nc.vector.tensor_scalar_max(out=lower[:], in0=out_sums[1][:], scalar1=0.0)
        nc.sync.dma_start(out=out[P : 2 * P, :], in_=lower[:])
